import numpy as np
import ml_dtypes


def mxq(x, axis, fmt="e4m3"):
    dtype, down = {"e4m3": (ml_dtypes.float8_e4m3fn, 7), "e5m2": (ml_dtypes.float8_e5m2, 14)}[fmt]
    v = np.moveaxis(np.asarray(x, np.float32).astype(ml_dtypes.bfloat16).astype(np.float64), axis, -1)
    blocks = v.reshape(v.shape[:-1] + (-1, 32))
    amax = np.abs(blocks).max(-1, keepdims=True)
    byte = np.maximum(np.where(amax > 0, np.frexp(amax)[1] - 1 + 127, 0) - down, 1)
    scale = np.exp2(byte - 127.0)
    codes = (blocks / scale).astype(np.float32).astype(dtype).astype(np.float64)
    return np.moveaxis((codes * scale).reshape(v.shape), -1, axis)


WIDE = False


def mx_kscale(k):
    if not WIDE:
        return np.ones(k)
    levels = np.array([10, -10, 5, -5, 0])
    if k % 512:
        return np.exp2(np.random.permutation(np.resize(levels, k // 32))).repeat(32)
    a = np.empty((k // 512, 16))
    for p in range(k // 512):
        a[p, :8] = np.random.permutation(np.resize(levels, 8))
        for g in range(8):
            far = levels[np.abs(levels - a[p, g]) >= 10]
            a[p, g + 8] = far[np.random.randint(len(far))]
    return np.exp2(a.ravel()).repeat(32)


def f64(x):
    return np.asarray(x).astype(np.float64)


def striped(idx):
    return np.tile(idx.reshape(-1, 16).T, (8, 1)).astype(np.uint16)


def unstriped(offs):
    return offs[:16].T.reshape(-1).astype(np.int64)


def relu(v):
    return np.maximum(v, 0.0)


K, T, E, C, N = 1024, 1024, 8, 128, 256


def by_expert(wq, xq):
    return np.concatenate([wq[e].T @ xq[:, e * C:(e + 1) * C] for e in range(E)], axis=1)


def setup_inputs():
    n = np.random.standard_normal
    s = mx_kscale(K)[:, None]
    return {
        "xT": (n((K, T)) * s).astype(np.float32),
        "w": (n((E, K, N)) / np.sqrt(K) / s[None]).astype(np.float32),
        "b": (0.3 * n((N, E))).astype(np.float32),
        "gate": np.tile(np.random.uniform(0.2, 1.0, E * C), (N, 1)).astype(np.float32),
        "offs": striped(np.random.permutation(T)[:E * C]),
        "dst": striped(np.random.permutation(T)[:E * C]),
    }


def reference(xT, w, b, gate, offs, dst):
    idx = unstriped(offs)
    xq = mxq(f64(xT)[:, idx], 0, "e4m3")
    y = by_expert(mxq(f64(w), 1, "e4m3"), xq)
    y = relu(y + np.repeat(f64(b), C, axis=1))
    out = np.zeros((N, T))
    out[:, unstriped(dst)] = f64(gate) * y
    return out

@@ -1,0 +1,197 @@
+from contextlib import ExitStack
+
+import concourse.mybir as mybir
+
+K, T, E, C, N = 1024, 1024, 8, 128, 256
+FLOPS = 2 * K * N * E * C
+
+F32 = mybir.dt.float32
+BF16 = mybir.dt.bfloat16
+U32 = mybir.dt.uint32
+U16 = mybir.dt.uint16
+U8 = mybir.dt.uint8
+FP8X4 = mybir.dt.float8_e4m3fn_x4
+COPY = mybir.ActivationFunctionType.Copy
+RELU = mybir.ActivationFunctionType.Relu
+MULT = mybir.AluOpType.mult
+
+P = 128
+PACK = 4
+PASSES = K // (P * PACK)
+HALVES = N // P
+
+
+def tile_moe_two_lin_relu_kernel(tc, xT, w, b, gate, offs, dst, out):
+    nc = tc.nc
+
+    def interleave(engine, grouped, raw):
+        to = grouped.rearrange("p (c i) t -> p c t i", i=4)
+        of = raw.rearrange("p t (c i) -> p c t i", i=4)
+        if engine == "v":
+            nc.vector.tensor_copy(out=to, in_=of)
+        else:
+            nc.scalar.activation(to, of, COPY)
+
+    with ExitStack() as ctx:
+        lists = ctx.enter_context(tc.tile_pool(name="lists", bufs=1))
+        keep = ctx.enter_context(tc.tile_pool(name="keep", bufs=1))
+        psum = ctx.enter_context(tc.psum_pool(name="psum", bufs=1))
+
+        offs_sb = lists.tile([P, E * C // 16], U16, name="offs_sb")
+        dst_sb = lists.tile([P, E * C // 16], U16, name="dst_sb")
+        gate_sb = [keep.tile([P, HALVES, E * C // 2], F32, name=f"gate_sb_{q}") for q in range(2)]
+        bias_sb = keep.tile([P, HALVES, E], F32, name="bias_sb")
+
+        CH = {0: [(0, 512), (512, 1024)], 1: [(0, 512), (512, 768), (768, 1024)]}
+        x_raw = {}
+        for c in range(PASSES):
+            for lo, hi in CH[c]:
+                x_raw[c, lo] = keep.tile([P, PACK, hi - lo], F32, name=f"x_raw_{c}_{lo}")
+        w_raw = [keep.tile([P, PASSES, PACK, N], F32, name=f"w_raw_{e}") for e in range(E)]
+
+        def load_x(c):
+            rows = xT[c * P * PACK : (c + 1) * P * PACK, :].rearrange("(p j) t -> p j t", j=PACK)
+            for lo, hi in CH[c]:
+                nc.sync.dma_start(out=x_raw[c, lo][:], in_=rows[:, :, lo:hi])
+
+        def load_w(e):
+            rows = w[e].rearrange("(c p j) n -> p c j n", p=P, j=PACK)
+            if e == E - 1:
+                for c in range(PASSES):
+                    nc.sync.dma_start(out=w_raw[e][:, c], in_=rows[:, c])
+            else:
+                nc.sync.dma_start(out=w_raw[e][:], in_=rows)
+
+        def load_gate(q):
+            cols = slice(q * E * C // 2, (q + 1) * E * C // 2)
+            nc.sync.dma_start(out=gate_sb[q][:], in_=gate[:, cols].rearrange("(h p) j -> p h j", p=P))
+
+        x_scales = keep.tile([P, T], U8, name="x_scales", align_bytes=64)
+        nc.gpsimd.memset(x_scales[:], 0)
+
+
+        load_x(0)
+        nc.sync.dma_start(offs_sb[:], offs)
+        load_x(1)
+        load_w(0)
+        nc.sync.dma_start(dst_sb[:], dst)
+        nc.sync.dma_start(out=bias_sb[:], in_=b.rearrange("(h p) e -> p h e", p=P))
+        load_w(1)
+        load_gate(0)
+        load_w(2)
+        load_w(3)
+        load_gate(1)
+        for e in range(4, E):
+            load_w(e)
+
+        x_bf = [keep.tile([P, T, PACK], BF16, name=f"x_bf_{c}", align_bytes=64) for c in range(PASSES)]
+        x_codes = [keep.tile([P, T], U32, name=f"x_codes_{c}", align_bytes=64) for c in range(PASSES)]
+        PIECES = [(0, 512), (512, 1024)]
+        g_codes = [[keep.tile([P, hi - lo], U32, name=f"g_codes_{c}_{lo}", align_bytes=64) for lo, hi in PIECES] for c in range(PASSES)]
+        g_scales = [[keep.tile([P, hi - lo], U8, name=f"g_scales_{c}_{lo}", align_bytes=64) for lo, hi in PIECES] for c in range(1)]
+        w_bf = [keep.tile([P, PASSES, N, PACK], BF16, name=f"w_bf_{e}", align_bytes=64) for e in range(E)]
+        w_codes = [keep.tile([P, PASSES, N], U32, name=f"w_codes_{e}", align_bytes=64) for e in range(E)]
+        w_scales = [keep.tile([P, PASSES, N], U8, name=f"w_scales_{e}", align_bytes=64) for e in range(E)]
+        y_sb = [[keep.tile([P, C], F32, name=f"y_{e}_{h}") for h in range(HALVES)] for e in range(E)]
+        acc = [psum.tile([P, HALVES, C], F32, name=f"acc_{e}") for e in range(E)]
+        out_sb = [keep.tile([P, T], F32, name=f"out_sb_{h}") for h in range(HALVES)]
+
+        def x_prep(c, lo, hi, v_cols):
+            if v_cols > 0:
+                interleave("v", x_bf[c][:, lo : lo + v_cols, :], x_raw[c, lo][:, :, 0:v_cols])
+            if v_cols < hi - lo:
+                interleave("s", x_bf[c][:, lo + v_cols : hi, :], x_raw[c, lo][:, :, v_cols : hi - lo])
+
+        def x_quant(c, lo, hi):
+            plane = x_scales[4 * c : P, lo:hi]
+            nc.vector.quantize_mx(out=x_codes[c][:, lo:hi].bitcast(FP8X4), scales=plane,
+                                  in_=x_bf[c][:, lo:hi, :].rearrange("p t j -> p (t j)"))
+
+        def offsets(i):
+            lo, hi = PIECES[i]
+            return offs_sb[:, lo // 16 : hi // 16]
+
+        def gather_codes(c, i):
+            nc.vector.tensor_copy(g_codes[c][i][:], x_codes[c][:].indirect(offsets(i)))
+
+        def gather_scales(c, i):
+            src = x_scales
+            nc.vector.tensor_copy(g_scales[c][i][:], src[:].indirect(offsets(i)))
+
+        W_ENG = [[0, 0]] * E
+
+        def w_prep(e):
+            for c in range(PASSES):
+                v_cols = W_ENG[e][c]
+                if v_cols > 0:
+                    interleave("v", w_bf[e][:, c, 0:v_cols], w_raw[e][:, c, :, 0:v_cols])
+                if v_cols < N:
+                    interleave("s", w_bf[e][:, c, v_cols:N], w_raw[e][:, c, :, v_cols:N])
+
+        def w_quant(e):
+            if e == E - 1:
+                for c in range(PASSES):
+                    nc.vector.quantize_mx(out=w_codes[e][:, c].bitcast(FP8X4), scales=w_scales[e][:, c],
+                                          in_=w_bf[e][:, c].rearrange("p n j -> p (n j)"))
+                return
+            nc.vector.quantize_mx(out=w_codes[e][:].rearrange("p c n -> p (c n)").bitcast(FP8X4),
+                                  scales=w_scales[e][:].rearrange("p c n -> p (c n)"),
+                                  in_=w_bf[e][:].rearrange("p c n j -> p (c n j)"))
+
+        def multiply(e):
+            i = [k for k in range(len(PIECES)) if PIECES[k][0] <= e * C < PIECES[k][1]][0]
+            cols = slice(e * C - PIECES[i][0], (e + 1) * C - PIECES[i][0])
+            for h in range(HALVES):
+                for c in range(PASSES):
+                    nc.tensor.matmul_mx(
+                        out=acc[e][:, h],
+                        lhsT=w_codes[e][:, c, h * P : (h + 1) * P].bitcast(FP8X4),
+                        lhsT_scale=w_scales[e][:, c, h * P : (h + 1) * P],
+                        rhs=g_codes[c][i][:, cols].bitcast(FP8X4),
+                        rhs_scale=g_scales[0][i][4 * c : P, cols],
+                        start=(c == 0),
+                        stop=(c == PASSES - 1),
+                    )
+
+        def leave(e):
+            for h in range(HALVES):
+                nc.scalar.activation(y_sb[e][h][:], acc[e][:, h], RELU, bias=bias_sb[:, h, e : e + 1])
+
+        def scatter(e):
+            for h in range(HALVES):
+                slots = slice(e % 4 * C, (e % 4 + 1) * C)
+                nc.vector.tensor_tensor(out_sb[h][:].indirect(dst_sb[:, e * C // 16 : (e + 1) * C // 16]),
+                                        y_sb[e][h][:], gate_sb[e // 4][:, h, slots], MULT)
+
+        XV = [[320, 320], [128, 64, 64]]
+        for k, (lo, hi) in enumerate(CH[0]):
+            x_prep(0, lo, hi, XV[0][k])
+            x_quant(0, lo, hi)
+        gather_codes(0, 0)
+        for k, (lo, hi) in enumerate(CH[1]):
+            x_prep(1, lo, hi, XV[1][k])
+            x_quant(1, lo, hi)
+            if k == 0:
+                gather_codes(0, 1)
+        gather_codes(1, 0)
+        gather_scales(0, 0)
+        w_prep(0)
+        w_quant(0)
+        gather_codes(1, 1)
+        multiply(0)
+        w_prep(1)
+        w_quant(1)
+        gather_scales(0, 1)
+        multiply(1)
+        for e in range(E):
+            if e + 2 < E:
+                w_prep(e + 2)
+            leave(e)
+            if e + 2 < E:
+                w_quant(e + 2)
+                multiply(e + 2)
+            scatter(e)
+
+
+        for h in range(HALVES):
+            nc.sync.dma_start(out=out[h * P : (h + 1) * P, :], in_=out_sb[h][:])

@@ -19,56 +19,67 @@ P = 128
 PACK = 4
 PASSES = K // (P * PACK)
 HALVES = N // P
+OFFSETS = 16
+RUN = 4
+
+PLANE_START = 4
+
+X_LOADS = [
+    [(0, 1024, 512)],
+    [(0, 512, 0), (512, 1024, 640)],
+]
+X_QUANTISED = [(0, 512), (512, 1024)]
+
+PARTS = [(0, 512), (512, 1024)]
+EARLY, LATE = 0, 1
+
+GATE_RANGES = [(0, 2), (2, 8)]
 
 
 def tile_moe_two_lin_relu_kernel(tc, xT, w, b, gate, offs, dst, out):
     nc = tc.nc
 
-    def interleave(engine, grouped, raw):
-        to = grouped.rearrange("p (c i) t -> p c t i", i=4)
-        of = raw.rearrange("p t (c i) -> p c t i", i=4)
-        if engine == "v":
-            nc.vector.tensor_copy(out=to, in_=of)
-        else:
-            nc.scalar.activation(to, of, COPY)
+    def interleaved_views(grouped, raw):
+        to = grouped.rearrange("p (c i) t -> p c t i", i=RUN)
+        of = raw.rearrange("p t (c i) -> p c t i", i=RUN)
+        return to, of
 
     with ExitStack() as ctx:
         lists = ctx.enter_context(tc.tile_pool(name="lists", bufs=1))
         keep = ctx.enter_context(tc.tile_pool(name="keep", bufs=1))
+        turn = ctx.enter_context(tc.tile_pool(name="turn", bufs=1))
         psum = ctx.enter_context(tc.psum_pool(name="psum", bufs=1))
 
-        offs_sb = lists.tile([P, E * C // 16], U16, name="offs_sb")
-        dst_sb = lists.tile([P, E * C // 16], U16, name="dst_sb")
-        gate_sb = [keep.tile([P, HALVES, E * C // 2], F32, name=f"gate_sb_{q}") for q in range(2)]
+        offs_sb = lists.tile([P, E * C // OFFSETS], U16, name="offs_sb")
+        dst_sb = lists.tile([P, E * C // OFFSETS], U16, name="dst_sb")
+        gate_sb = [
+            keep.tile([P, HALVES, (end - first) * C], F32, name=f"gate_sb_{first}")
+            for first, end in GATE_RANGES
+        ]
         bias_sb = keep.tile([P, HALVES, E], F32, name="bias_sb")
 
-        CH = {0: [(0, 512), (512, 1024)], 1: [(0, 512), (512, 768), (768, 1024)]}
-        x_raw = {}
-        for c in range(PASSES):
-            for lo, hi in CH[c]:
-                x_raw[c, lo] = keep.tile([P, PACK, hi - lo], F32, name=f"x_raw_{c}_{lo}")
+        x_raw = [
+            [keep.tile([P, PACK, end - first], F32, name=f"x_raw_{c}_{first}") for first, end, split in X_LOADS[c]]
+            for c in range(PASSES)
+        ]
         w_raw = [keep.tile([P, PASSES, PACK, N], F32, name=f"w_raw_{e}") for e in range(E)]
-
-        def load_x(c):
-            rows = xT[c * P * PACK : (c + 1) * P * PACK, :].rearrange("(p j) t -> p j t", j=PACK)
-            for lo, hi in CH[c]:
-                nc.sync.dma_start(out=x_raw[c, lo][:], in_=rows[:, :, lo:hi])
-
-        def load_w(e):
-            rows = w[e].rearrange("(c p j) n -> p c j n", p=P, j=PACK)
-            if e == E - 1:
-                for c in range(PASSES):
-                    nc.sync.dma_start(out=w_raw[e][:, c], in_=rows[:, c])
-            else:
-                nc.sync.dma_start(out=w_raw[e][:], in_=rows)
-
-        def load_gate(q):
-            cols = slice(q * E * C // 2, (q + 1) * E * C // 2)
-            nc.sync.dma_start(out=gate_sb[q][:], in_=gate[:, cols].rearrange("(h p) j -> p h j", p=P))
 
         x_scales = keep.tile([P, T], U8, name="x_scales", align_bytes=64)
         nc.gpsimd.memset(x_scales[:], 0)
 
+        def load_x(c):
+            rows = xT[c * P * PACK : (c + 1) * P * PACK, :].rearrange("(p j) t -> p j t", j=PACK)
+            for tile, (first, end, split) in zip(x_raw[c], X_LOADS[c]):
+                nc.sync.dma_start(out=tile[:], in_=rows[:, :, first:end])
+
+        def load_w(e):
+            rows = w[e].rearrange("(c p j) n -> p c j n", p=P, j=PACK)
+            nc.sync.dma_start(out=w_raw[e][:], in_=rows)
+
+        def load_gate(g):
+            first, end = GATE_RANGES[g]
+            columns = gate[:, first * C : end * C].rearrange("(h p) j -> p h j", p=P)
+            nc.sync.dma_start(out=gate_sb[g][:], in_=columns)
 
         load_x(0)
         nc.sync.dma_start(offs_sb[:], offs)
@@ -86,112 +97,143 @@ def tile_moe_two_lin_relu_kernel(tc, xT, w, b, gate, offs, dst, out):
 
         x_bf = [keep.tile([P, T, PACK], BF16, name=f"x_bf_{c}", align_bytes=64) for c in range(PASSES)]
         x_codes = [keep.tile([P, T], U32, name=f"x_codes_{c}", align_bytes=64) for c in range(PASSES)]
-        PIECES = [(0, 512), (512, 1024)]
-        g_codes = [[keep.tile([P, hi - lo], U32, name=f"g_codes_{c}_{lo}", align_bytes=64) for lo, hi in PIECES] for c in range(PASSES)]
-        g_scales = [[keep.tile([P, hi - lo], U8, name=f"g_scales_{c}_{lo}", align_bytes=64) for lo, hi in PIECES] for c in range(1)]
-        w_bf = [keep.tile([P, PASSES, N, PACK], BF16, name=f"w_bf_{e}", align_bytes=64) for e in range(E)]
+
+        g_codes = [
+            [
+                keep.tile([P, end - first], U32, name=f"g_codes_{c}_{first}", align_bytes=64)
+                for first, end in PARTS[: PASSES - c]
+            ]
+            for c in range(PASSES)
+        ]
+        g_scales = [keep.tile([P, PARTS[EARLY][1]], U8, name="g_scales_0", align_bytes=64)]
+
+        w_first = [
+            turn.tile([P, N, PACK], BF16, name=f"w_first_{c}", tag=f"turn_{c}", align_bytes=64)
+            for c in range(PASSES)
+        ]
+        w_bf = {e: keep.tile([P, PASSES, N, PACK], BF16, name=f"w_bf_{e}", align_bytes=64) for e in range(1, E)}
         w_codes = [keep.tile([P, PASSES, N], U32, name=f"w_codes_{e}", align_bytes=64) for e in range(E)]
         w_scales = [keep.tile([P, PASSES, N], U8, name=f"w_scales_{e}", align_bytes=64) for e in range(E)]
-        y_sb = [[keep.tile([P, C], F32, name=f"y_{e}_{h}") for h in range(HALVES)] for e in range(E)]
-        acc = [psum.tile([P, HALVES, C], F32, name=f"acc_{e}") for e in range(E)]
+
+        y_last = keep.tile([P, HALVES, C], F32, name="y_last")
+        y = [[w_raw[e + 1][:, 0, h, 0:C] for h in range(HALVES)] for e in range(E - 1)]
+        y.append([y_last[:, h] for h in range(HALVES)])
+
+        acc = [psum.tile([P, HALVES, C], F32, name=f"acc_{e}", tag=f"bank_{e}") for e in range(E)]
         out_sb = [keep.tile([P, T], F32, name=f"out_sb_{h}") for h in range(HALVES)]
 
-        def x_prep(c, lo, hi, v_cols):
-            if v_cols > 0:
-                interleave("v", x_bf[c][:, lo : lo + v_cols, :], x_raw[c, lo][:, :, 0:v_cols])
-            if v_cols < hi - lo:
-                interleave("s", x_bf[c][:, lo + v_cols : hi, :], x_raw[c, lo][:, :, v_cols : hi - lo])
+        def interleave_x(c, load):
+            first, end, split = X_LOADS[c][load]
+            raw = x_raw[c][load]
+            if split > first:
+                to, of = interleaved_views(x_bf[c][:, first:split, :], raw[:, :, 0 : split - first])
+                nc.vector.tensor_copy(out=to, in_=of)
+            scalar_first = max(first, split)
+            to, of = interleaved_views(x_bf[c][:, scalar_first:end, :], raw[:, :, scalar_first - first : end - first])
+            nc.scalar.activation(to, of, COPY)
 
-        def x_quant(c, lo, hi):
-            plane = x_scales[4 * c : P, lo:hi]
-            nc.vector.quantize_mx(out=x_codes[c][:, lo:hi].bitcast(FP8X4), scales=plane,
-                                  in_=x_bf[c][:, lo:hi, :].rearrange("p t j -> p (t j)"))
+        def quantise_x(c, first, end):
+            nc.vector.quantize_mx(
+                out=x_codes[c][:, first:end].bitcast(FP8X4),
+                scales=x_scales[PLANE_START * c : P, first:end],
+                in_=x_bf[c][:, first:end, :].rearrange("p t j -> p (t j)"),
+            )
 
-        def offsets(i):
-            lo, hi = PIECES[i]
-            return offs_sb[:, lo // 16 : hi // 16]
+        def part_offsets(part):
+            first, end = PARTS[part]
+            return offs_sb[:, first // OFFSETS : end // OFFSETS]
 
-        def gather_codes(c, i):
-            nc.vector.tensor_copy(g_codes[c][i][:], x_codes[c][:].indirect(offsets(i)))
+        def gather_codes(c, part):
+            nc.vector.tensor_copy(g_codes[c][part][:], x_codes[c][:].indirect(part_offsets(part)))
 
-        def gather_scales(c, i):
-            src = x_scales
-            nc.vector.tensor_copy(g_scales[c][i][:], src[:].indirect(offsets(i)))
+        def gather_scales(part):
+            nc.vector.tensor_copy(g_scales[part][:], x_scales[:].indirect(part_offsets(part)))
 
-        W_ENG = [[0, 0]] * E
+        def interleave_w(e, c):
+            grouped = w_first[c][:] if e == 0 else w_bf[e][:, c]
+            to, of = interleaved_views(grouped, w_raw[e][:, c])
+            nc.scalar.activation(to, of, COPY)
 
-        def w_prep(e):
+        def quantise_first_w():
             for c in range(PASSES):
-                v_cols = W_ENG[e][c]
-                if v_cols > 0:
-                    interleave("v", w_bf[e][:, c, 0:v_cols], w_raw[e][:, c, :, 0:v_cols])
-                if v_cols < N:
-                    interleave("s", w_bf[e][:, c, v_cols:N], w_raw[e][:, c, :, v_cols:N])
+                nc.vector.quantize_mx(
+                    out=w_codes[0][:, c].bitcast(FP8X4),
+                    scales=w_scales[0][:, c],
+                    in_=w_first[c][:].rearrange("p n j -> p (n j)"),
+                )
 
-        def w_quant(e):
-            if e == E - 1:
-                for c in range(PASSES):
-                    nc.vector.quantize_mx(out=w_codes[e][:, c].bitcast(FP8X4), scales=w_scales[e][:, c],
-                                          in_=w_bf[e][:, c].rearrange("p n j -> p (n j)"))
-                return
-            nc.vector.quantize_mx(out=w_codes[e][:].rearrange("p c n -> p (c n)").bitcast(FP8X4),
-                                  scales=w_scales[e][:].rearrange("p c n -> p (c n)"),
-                                  in_=w_bf[e][:].rearrange("p c n j -> p (c n j)"))
+        def quantise_w(e):
+            nc.vector.quantize_mx(
+                out=w_codes[e][:].rearrange("p c n -> p (c n)").bitcast(FP8X4),
+                scales=w_scales[e][:].rearrange("p c n -> p (c n)"),
+                in_=w_bf[e][:].rearrange("p c n j -> p (c n j)"),
+            )
 
         def multiply(e):
-            i = [k for k in range(len(PIECES)) if PIECES[k][0] <= e * C < PIECES[k][1]][0]
-            cols = slice(e * C - PIECES[i][0], (e + 1) * C - PIECES[i][0])
+            part = EARLY if e * C < PARTS[EARLY][1] else LATE
+            slots = slice(e * C - PARTS[part][0], (e + 1) * C - PARTS[part][0])
             for h in range(HALVES):
+                channels = slice(h * P, (h + 1) * P)
                 for c in range(PASSES):
                     nc.tensor.matmul_mx(
                         out=acc[e][:, h],
-                        lhsT=w_codes[e][:, c, h * P : (h + 1) * P].bitcast(FP8X4),
-                        lhsT_scale=w_scales[e][:, c, h * P : (h + 1) * P],
-                        rhs=g_codes[c][i][:, cols].bitcast(FP8X4),
-                        rhs_scale=g_scales[0][i][4 * c : P, cols],
+                        lhsT=w_codes[e][:, c, channels].bitcast(FP8X4),
+                        lhsT_scale=w_scales[e][:, c, channels],
+                        rhs=g_codes[c][part][:, slots].bitcast(FP8X4),
+                        rhs_scale=g_scales[part][PLANE_START * c : P, slots],
                         start=(c == 0),
                         stop=(c == PASSES - 1),
                     )
 
-        def leave(e):
+        def add_bias_and_relu(e):
             for h in range(HALVES):
-                nc.scalar.activation(y_sb[e][h][:], acc[e][:, h], RELU, bias=bias_sb[:, h, e : e + 1])
+                nc.scalar.activation(y[e][h], acc[e][:, h], RELU, bias=bias_sb[:, h, e : e + 1])
 
         def scatter(e):
+            g = [r for r, (first, end) in enumerate(GATE_RANGES) if first <= e < end][0]
+            first = (e - GATE_RANGES[g][0]) * C
+            places = dst_sb[:, e * C // OFFSETS : (e + 1) * C // OFFSETS]
             for h in range(HALVES):
-                slots = slice(e % 4 * C, (e % 4 + 1) * C)
-                nc.vector.tensor_tensor(out_sb[h][:].indirect(dst_sb[:, e * C // 16 : (e + 1) * C // 16]),
-                                        y_sb[e][h][:], gate_sb[e // 4][:, h, slots], MULT)
+                nc.vector.tensor_tensor(
+                    out_sb[h][:].indirect(places), y[e][h], gate_sb[g][:, h, first : first + C], MULT
+                )
 
-        XV = [[320, 320], [128, 64, 64]]
-        for k, (lo, hi) in enumerate(CH[0]):
-            x_prep(0, lo, hi, XV[0][k])
-            x_quant(0, lo, hi)
-        gather_codes(0, 0)
-        for k, (lo, hi) in enumerate(CH[1]):
-            x_prep(1, lo, hi, XV[1][k])
-            x_quant(1, lo, hi)
-            if k == 0:
-                gather_codes(0, 1)
-        gather_codes(1, 0)
-        gather_scales(0, 0)
-        w_prep(0)
-        w_quant(0)
-        gather_codes(1, 1)
+        interleave_x(0, 0)
+        for first, end in X_QUANTISED:
+            quantise_x(0, first, end)
+        gather_codes(0, EARLY)
+        gather_codes(0, LATE)
+        for load, (first, end, split) in enumerate(X_LOADS[1]):
+            interleave_x(1, load)
+            quantise_x(1, first, end)
+        gather_codes(1, EARLY)
+        gather_scales(EARLY)
+
+        for c in range(PASSES):
+            interleave_w(0, c)
+        quantise_first_w()
         multiply(0)
-        w_prep(1)
-        w_quant(1)
-        gather_scales(0, 1)
-        multiply(1)
-        for e in range(E):
-            if e + 2 < E:
-                w_prep(e + 2)
-            leave(e)
-            if e + 2 < E:
-                w_quant(e + 2)
-                multiply(e + 2)
-            scatter(e)
 
+        g_codes_late = turn.tile(
+            [P, PARTS[LATE][1] - PARTS[LATE][0]], U32, name="g_codes_late", tag="turn_0", align_bytes=64
+        )
+        g_codes[1].append(g_codes_late)
+        gather_codes(1, LATE)
+        g_scales_late = turn.tile(
+            [P, PARTS[LATE][1] - PARTS[LATE][0]], U8, name="g_scales_late", tag="turn_1", align_bytes=64
+        )
+        g_scales.append(g_scales_late)
+        gather_scales(LATE)
+
+        for e in range(E):
+            if e + 1 < E:
+                interleave_w(e + 1, 0)
+            add_bias_and_relu(e)
+            if e + 1 < E:
+                interleave_w(e + 1, 1)
+                quantise_w(e + 1)
+                multiply(e + 1)
+            scatter(e)
 
         for h in range(HALVES):
             nc.sync.dma_start(out=out[h * P : (h + 1) * P, :], in_=out_sb[h][:])

from contextlib import ExitStack

import concourse.mybir as mybir

K, T, E, C, N = 1024, 1024, 8, 128, 256
FLOPS = 2 * K * N * E * C

F32 = mybir.dt.float32
BF16 = mybir.dt.bfloat16
U32 = mybir.dt.uint32
U16 = mybir.dt.uint16
U8 = mybir.dt.uint8
FP8X4 = mybir.dt.float8_e4m3fn_x4
COPY = mybir.ActivationFunctionType.Copy
RELU = mybir.ActivationFunctionType.Relu
MULT = mybir.AluOpType.mult

P = 128
PACK = 4
PASSES = K // (P * PACK)
HALVES = N // P
OFFSETS = 16
RUN = 4

PLANE_START = 4

X_LOADS = [
    [(0, 1024, 512)],
    [(0, 512, 0), (512, 1024, 640)],
]
X_QUANTISED = [(0, 512), (512, 1024)]

PARTS = [(0, 512), (512, 1024)]
EARLY, LATE = 0, 1

GATE_RANGES = [(0, 2), (2, 8)]


def tile_moe_two_lin_relu_kernel(tc, xT, w, b, gate, offs, dst, out):
    nc = tc.nc

    def interleaved_views(grouped, raw):
        to = grouped.rearrange("p (c i) t -> p c t i", i=RUN)
        of = raw.rearrange("p t (c i) -> p c t i", i=RUN)
        return to, of

    with ExitStack() as ctx:
        lists = ctx.enter_context(tc.tile_pool(name="lists", bufs=1))
        keep = ctx.enter_context(tc.tile_pool(name="keep", bufs=1))
        turn = ctx.enter_context(tc.tile_pool(name="turn", bufs=1))
        psum = ctx.enter_context(tc.psum_pool(name="psum", bufs=1))

        offs_sb = lists.tile([P, E * C // OFFSETS], U16, name="offs_sb")
        dst_sb = lists.tile([P, E * C // OFFSETS], U16, name="dst_sb")
        gate_sb = [
            keep.tile([P, HALVES, (end - first) * C], F32, name=f"gate_sb_{first}")
            for first, end in GATE_RANGES
        ]
        bias_sb = keep.tile([P, HALVES, E], F32, name="bias_sb")

        x_raw = [
            [keep.tile([P, PACK, end - first], F32, name=f"x_raw_{c}_{first}") for first, end, split in X_LOADS[c]]
            for c in range(PASSES)
        ]
        w_raw = [keep.tile([P, PASSES, PACK, N], F32, name=f"w_raw_{e}") for e in range(E)]

        x_scales = keep.tile([P, T], U8, name="x_scales", align_bytes=64)
        nc.gpsimd.memset(x_scales[:], 0)

        def load_x(c):
            rows = xT[c * P * PACK : (c + 1) * P * PACK, :].rearrange("(p j) t -> p j t", j=PACK)
            for tile, (first, end, split) in zip(x_raw[c], X_LOADS[c]):
                nc.sync.dma_start(out=tile[:], in_=rows[:, :, first:end])

        def load_w(e):
            rows = w[e].rearrange("(c p j) n -> p c j n", p=P, j=PACK)
            nc.sync.dma_start(out=w_raw[e][:], in_=rows)

        def load_gate(g):
            first, end = GATE_RANGES[g]
            columns = gate[:, first * C : end * C].rearrange("(h p) j -> p h j", p=P)
            nc.sync.dma_start(out=gate_sb[g][:], in_=columns)

        load_x(0)
        nc.sync.dma_start(offs_sb[:], offs)
        load_x(1)
        load_w(0)
        nc.sync.dma_start(dst_sb[:], dst)
        nc.sync.dma_start(out=bias_sb[:], in_=b.rearrange("(h p) e -> p h e", p=P))
        load_w(1)
        load_gate(0)
        load_w(2)
        load_w(3)
        load_gate(1)
        for e in range(4, E):
            load_w(e)

        x_bf = [keep.tile([P, T, PACK], BF16, name=f"x_bf_{c}", align_bytes=64) for c in range(PASSES)]
        x_codes = [keep.tile([P, T], U32, name=f"x_codes_{c}", align_bytes=64) for c in range(PASSES)]

        g_codes = [
            [
                keep.tile([P, end - first], U32, name=f"g_codes_{c}_{first}", align_bytes=64)
                for first, end in PARTS[: PASSES - c]
            ]
            for c in range(PASSES)
        ]
        g_scales = [keep.tile([P, PARTS[EARLY][1]], U8, name="g_scales_0", align_bytes=64)]

        w_first = [
            turn.tile([P, N, PACK], BF16, name=f"w_first_{c}", tag=f"turn_{c}", align_bytes=64)
            for c in range(PASSES)
        ]
        w_bf = {e: keep.tile([P, PASSES, N, PACK], BF16, name=f"w_bf_{e}", align_bytes=64) for e in range(1, E)}
        w_codes = [keep.tile([P, PASSES, N], U32, name=f"w_codes_{e}", align_bytes=64) for e in range(E)]
        w_scales = [keep.tile([P, PASSES, N], U8, name=f"w_scales_{e}", align_bytes=64) for e in range(E)]

        y_last = keep.tile([P, HALVES, C], F32, name="y_last")
        y = [[w_raw[e + 1][:, 0, h, 0:C] for h in range(HALVES)] for e in range(E - 1)]
        y.append([y_last[:, h] for h in range(HALVES)])

        acc = [psum.tile([P, HALVES, C], F32, name=f"acc_{e}", tag=f"bank_{e}") for e in range(E)]
        out_sb = [keep.tile([P, T], F32, name=f"out_sb_{h}") for h in range(HALVES)]

        def interleave_x(c, load):
            first, end, split = X_LOADS[c][load]
            raw = x_raw[c][load]
            if split > first:
                to, of = interleaved_views(x_bf[c][:, first:split, :], raw[:, :, 0 : split - first])
                nc.vector.tensor_copy(out=to, in_=of)
            scalar_first = max(first, split)
            to, of = interleaved_views(x_bf[c][:, scalar_first:end, :], raw[:, :, scalar_first - first : end - first])
            nc.scalar.activation(to, of, COPY)

        def quantise_x(c, first, end):
            nc.vector.quantize_mx(
                out=x_codes[c][:, first:end].bitcast(FP8X4),
                scales=x_scales[PLANE_START * c : P, first:end],
                in_=x_bf[c][:, first:end, :].rearrange("p t j -> p (t j)"),
            )

        def part_offsets(part):
            first, end = PARTS[part]
            return offs_sb[:, first // OFFSETS : end // OFFSETS]

        def gather_codes(c, part):
            nc.vector.tensor_copy(g_codes[c][part][:], x_codes[c][:].indirect(part_offsets(part)))

        def gather_scales(part):
            nc.vector.tensor_copy(g_scales[part][:], x_scales[:].indirect(part_offsets(part)))

        def interleave_w(e, c):
            grouped = w_first[c][:] if e == 0 else w_bf[e][:, c]
            to, of = interleaved_views(grouped, w_raw[e][:, c])
            nc.scalar.activation(to, of, COPY)

        def quantise_first_w():
            for c in range(PASSES):
                nc.vector.quantize_mx(
                    out=w_codes[0][:, c].bitcast(FP8X4),
                    scales=w_scales[0][:, c],
                    in_=w_first[c][:].rearrange("p n j -> p (n j)"),
                )

        def quantise_w(e):
            nc.vector.quantize_mx(
                out=w_codes[e][:].rearrange("p c n -> p (c n)").bitcast(FP8X4),
                scales=w_scales[e][:].rearrange("p c n -> p (c n)"),
                in_=w_bf[e][:].rearrange("p c n j -> p (c n j)"),
            )

        def multiply(e):
            part = EARLY if e * C < PARTS[EARLY][1] else LATE
            slots = slice(e * C - PARTS[part][0], (e + 1) * C - PARTS[part][0])
            for h in range(HALVES):
                channels = slice(h * P, (h + 1) * P)
                for c in range(PASSES):
                    nc.tensor.matmul_mx(
                        out=acc[e][:, h],
                        lhsT=w_codes[e][:, c, channels].bitcast(FP8X4),
                        lhsT_scale=w_scales[e][:, c, channels],
                        rhs=g_codes[c][part][:, slots].bitcast(FP8X4),
                        rhs_scale=g_scales[part][PLANE_START * c : P, slots],
                        start=(c == 0),
                        stop=(c == PASSES - 1),
                    )

        def add_bias_and_relu(e):
            for h in range(HALVES):
                nc.scalar.activation(y[e][h], acc[e][:, h], RELU, bias=bias_sb[:, h, e : e + 1])

        def scatter(e):
            g = [r for r, (first, end) in enumerate(GATE_RANGES) if first <= e < end][0]
            first = (e - GATE_RANGES[g][0]) * C
            places = dst_sb[:, e * C // OFFSETS : (e + 1) * C // OFFSETS]
            for h in range(HALVES):
                nc.vector.tensor_tensor(
                    out_sb[h][:].indirect(places), y[e][h], gate_sb[g][:, h, first : first + C], MULT
                )

        interleave_x(0, 0)
        for first, end in X_QUANTISED:
            quantise_x(0, first, end)
        gather_codes(0, EARLY)
        gather_codes(0, LATE)
        for load, (first, end, split) in enumerate(X_LOADS[1]):
            interleave_x(1, load)
            quantise_x(1, first, end)
        gather_codes(1, EARLY)
        gather_scales(EARLY)

        for c in range(PASSES):
            interleave_w(0, c)
        quantise_first_w()
        multiply(0)

        g_codes_late = turn.tile(
            [P, PARTS[LATE][1] - PARTS[LATE][0]], U32, name="g_codes_late", tag="turn_0", align_bytes=64
        )
        g_codes[1].append(g_codes_late)
        gather_codes(1, LATE)
        g_scales_late = turn.tile(
            [P, PARTS[LATE][1] - PARTS[LATE][0]], U8, name="g_scales_late", tag="turn_1", align_bytes=64
        )
        g_scales.append(g_scales_late)
        gather_scales(LATE)

        for e in range(E):
            if e + 1 < E:
                interleave_w(e + 1, 0)
            add_bias_and_relu(e)
            if e + 1 < E:
                interleave_w(e + 1, 1)
                quantise_w(e + 1)
                multiply(e + 1)
            scatter(e)

        for h in range(HALVES):
            nc.sync.dma_start(out=out[h * P : (h + 1) * P, :], in_=out_sb[h][:])
